import numpy as np
import ml_dtypes


def mxq(x, axis, fmt="e4m3"):
    dtype, down = {"e4m3": (ml_dtypes.float8_e4m3fn, 7), "e5m2": (ml_dtypes.float8_e5m2, 14)}[fmt]
    v = np.moveaxis(np.asarray(x, np.float32).astype(ml_dtypes.bfloat16).astype(np.float64), axis, -1)
    blocks = v.reshape(v.shape[:-1] + (-1, 32))
    amax = np.abs(blocks).max(-1, keepdims=True)
    byte = np.maximum(np.where(amax > 0, np.frexp(amax)[1] - 1 + 127, 0) - down, 1)
    scale = np.exp2(byte - 127.0)
    codes = (blocks / scale).astype(np.float32).astype(dtype).astype(np.float64)
    return np.moveaxis((codes * scale).reshape(v.shape), -1, axis)


WIDE = False


def mx_kscale(k):
    if not WIDE:
        return np.ones(k)
    levels = np.array([30, -30])
    if k % 512:
        return np.exp2(np.random.permutation(np.resize(levels, k // 32))).repeat(32)
    a = np.empty((k // 512, 16))
    for p in range(k // 512):
        a[p, :8] = np.random.permutation(np.resize(levels, 8))
        for g in range(8):
            far = levels[np.abs(levels - a[p, g]) >= 10]
            a[p, g + 8] = far[np.random.randint(len(far))]
    return np.exp2(a.ravel()).repeat(32)


def f64(x):
    return np.asarray(x).astype(np.float64)


def striped(idx):
    return np.tile(np.asarray(idx).reshape(-1, 16).T, (8, 1)).astype(np.uint16)


def unstriped(offs):
    return offs[:16].T.reshape(-1).astype(np.int64)


E2M1 = np.array([0.0, 0.5, 1.0, 1.5, 2.0, 3.0, 4.0, 6.0, -0.0, -0.5, -1.0, -1.5, -2.0, -3.0, -4.0, -6.0])


def pack_weight(w, fmt):
    k, n = w.shape
    w = f64(np.asarray(w, np.float32).astype(ml_dtypes.bfloat16)).reshape(k // 32, 32, n)
    amax = np.abs(w).max(1)
    if fmt == "e4m3":
        byte = np.frexp(amax)[1] - 1 + 127 - 7
    else:
        mant, ex = np.frexp(amax / 6.0)
        byte = np.where(mant > 0.5, ex, ex - 1) + 127
    byte = np.clip(np.where(amax > 0, byte, 1), 1, 254)
    scaled = (w * np.exp2(127.0 - byte)[:, None, :]).reshape(k, n).astype(np.float32)
    by_word = np.ascontiguousarray(scaled.reshape(k // 512, 128, 4, n).transpose(0, 1, 3, 2))
    if fmt == "e4m3":
        words = by_word.astype(ml_dtypes.float8_e4m3fn).view(np.uint8)
    else:
        c = by_word.astype(ml_dtypes.float4_e2m1fn).view(np.uint8) & 0xF
        words = (c[..., 0::2] | (c[..., 1::2] << 4)).reshape(k // 512, 128, 2 * n)
    return np.ascontiguousarray(words), np.ascontiguousarray(byte.astype(np.uint8).reshape(k // 512, 16, n))


def unpack_weight(words, scales, fmt):
    g, _, n = scales.shape
    words = np.ascontiguousarray(words).reshape(g, 128, n, -1)
    if fmt == "e4m3":
        vals = words.view(ml_dtypes.float8_e4m3fn).astype(np.float64)
    else:
        nib = np.empty((g, 128, n, 4), np.uint8)
        nib[..., 0::2] = words & 0xF
        nib[..., 1::2] = words >> 4
        vals = E2M1[nib]
    vals = vals * np.repeat(np.exp2(scales.astype(np.float64) - 127.0), 8, axis=1)[..., None]
    return vals.transpose(0, 1, 3, 2).reshape(g * 512, n)


K, T, Z, J, R, C, O, N = 512, 1024, 1024, 256, 512, 512, 256, 256


def setup_inputs():
    n = np.random.standard_normal
    idx = np.random.permutation(T)[:J]
    idx2 = np.random.permutation(Z)[:J]
    idx3 = np.random.permutation(C)[:J]
    idx4 = np.random.permutation(C)[:J]
    idx5 = np.random.permutation(C)[:O]
    fk = mx_kscale(K)
    fr = mx_kscale(R)
    xtp = pack_weight(n((K, T)) / fk[:, None], "e2m1")
    xop = pack_weight(n((K, Z)) / fk[:, None], "e4m3")
    wp = pack_weight(n((K, R)) * 1 / np.sqrt(K) * fk[:, None] * fr, "e4m3")
    wbp = pack_weight(n((R, N)) * 1 / np.sqrt(R) / fr[:, None], "e2m1")
    return {
        "xt_words": xtp[0],
        "xt_scales": xtp[1],
        "xo_words": xop[0],
        "xo_scales": xop[1],
        "w_words": wp[0],
        "w_scales": wp[1],
        "wb_words": wbp[0],
        "wb_scales": wbp[1],
        "offs": striped(idx),
        "offs2": striped(idx2),
        "offs3": striped(idx3),
        "offs4": striped(idx4),
        "offs5": striped(idx5),
    }


def reference(xt_words, xt_scales, xo_words, xo_scales, w_words, w_scales, wb_words, wb_scales, offs, offs2, offs3, offs4, offs5):
    idx = unstriped(offs)
    idx2 = unstriped(offs2)
    idx3 = unstriped(offs3)
    idx4 = unstriped(offs4)
    idx5 = unstriped(offs5)
    xtu = unpack_weight(xt_words, xt_scales, "e2m1")
    xou = unpack_weight(xo_words, xo_scales, "e4m3")
    wu = unpack_weight(w_words, w_scales, "e4m3")
    wbu = unpack_weight(wb_words, wb_scales, "e2m1")
    xtidxg = xtu[:, idx]
    a = wu.T @ xtidxg
    xoidx2g = xou[:, idx2]
    b = wu.T @ xoidx2g
    pw = np.zeros((R, C))
    pw[:, idx3] = a
    pv = np.zeros((R, C))
    pv[:, idx4] = b
    pg = pw + pv
    hid = pg[:, idx5]
    hidq = mxq(hid, 0, "e5m2")
    y = wbu.T @ hidq
    return y

@@ -1,0 +1,150 @@
+from contextlib import ExitStack
+
+import concourse.mybir as mybir
+
+K, T, Z, J, R, C, O, N = 512, 1024, 1024, 256, 512, 512, 256, 256
+FLOPS = 2 * K * R * J * 2 + 2 * R * N * O
+
+F32 = mybir.dt.float32
+BF16 = mybir.dt.bfloat16
+I32 = mybir.dt.int32
+U32 = mybir.dt.uint32
+U16 = mybir.dt.uint16
+U8 = mybir.dt.uint8
+E4M3 = mybir.dt.float8_e4m3fn_x4
+E5M2 = mybir.dt.float8_e5m2_x4
+E2M1 = mybir.dt.float4_e2m1fn_x4
+COPY = mybir.ActivationFunctionType.Copy
+ADD = mybir.AluOpType.add
+
+P = 128
+PACK = 4
+
+
+def tile_list_oneforboth_shared_one_plain_kernel(
+    tc, xt_words, xt_scales, xo_words, xo_scales, w_words, w_scales, wb_words, wb_scales,
+    offs, offs2, offs3, offs4, offs5, out,
+):
+    nc = tc.nc
+    with ExitStack() as ctx:
+        keep = ctx.enter_context(tc.tile_pool(name="keep", bufs=1))
+        psum = ctx.enter_context(tc.psum_pool(name="psum", bufs=1))
+
+        def sb(name, shape, dtype):
+            return keep.tile(shape, dtype, name=name, align_bytes=64)
+
+        def load_list(name, src):
+            tile = sb(name, [P, J // 16], U16)
+            nc.sync.dma_start(tile[:], src)
+            return tile
+
+        def new_plane(name, width):
+            plane = sb(name, [P, width], U8)
+            nc.vector.memset(plane[:].bitcast(I32), 0)
+            return plane
+
+        def load_rows(queue, plane, src, r):
+            queue.dma_start(plane[r:P:32, :].bitcast(I32), src[0, r:16:4, :].bitcast(I32))
+
+        xt_s = new_plane("xt_s", T)
+        w_s = new_plane("w_s", R)
+        xo_s = new_plane("xo_s", Z)
+        wb_s = new_plane("wb_s", N)
+        xt_w = sb("xt_w", [P, T], U16)
+        w_w = sb("w_w", [P, R], U32)
+        xo_w = sb("xo_w", [P, Z], U32)
+        wb_w = sb("wb_w", [P, 2 * N], U8)
+
+        nc.sync.dma_start(xt_w[:].bitcast(I32), xt_words[0].bitcast(I32))
+        l1 = load_list("l1", offs)
+        nc.sync.dma_start(w_w[:].bitcast(I32), w_words[0].rearrange("p n t -> p (n t)").bitcast(I32))
+        for r in range(4):
+            load_rows(nc.scalar if r % 2 else nc.sync, xt_s, xt_scales, r)
+        for r in range(4):
+            load_rows(nc.scalar if r % 2 else nc.sync, w_s, w_scales, r)
+        l2 = load_list("l2", offs2)
+        nc.sync.dma_start(xo_w[:].bitcast(I32), xo_words[0].rearrange("p n t -> p (n t)").bitcast(I32))
+        l3 = load_list("l3", offs3)
+        for r in range(4):
+            load_rows(nc.sync, xo_s, xo_scales, r)
+        l4 = load_list("l4", offs4)
+        l5 = load_list("l5", offs5)
+        nc.sync.dma_start(wb_w[:].bitcast(I32), wb_words[0].bitcast(I32))
+        for r in range(4):
+            load_rows(nc.sync, wb_s, wb_scales, r)
+
+        pw = [sb("pw%d" % t, [P, C], F32) for t in range(PACK)]
+        pv = [sb("pv%d" % t, [P, C], F32) for t in range(PACK)]
+        for t in range(PACK):
+            nc.vector.memset(pw[t][:], 0.0)
+            nc.vector.memset(pv[t][:], 0.0)
+
+        wp_w = sb("wp_w", [P, R], U32)
+        wp_s = sb("wp_s", [P, R], U8)
+        gt_w = sb("gt_w", [P, J], U16)
+        gt_s = sb("gt_s", [P, J], U8)
+        go_w = sb("go_w", [P, J], U32)
+        go_s = sb("go_s", [P, J], U8)
+        nc.scalar.copy(wp_w[:].rearrange("p (t q) -> p t q", t=PACK), w_w[:].rearrange("p (q t) -> p t q", t=PACK))
+        nc.vector.tensor_copy(gt_w[:], xt_w[:].indirect(l1[:]))
+        nc.vector.tensor_copy(gt_s[:], xt_s[:].indirect(l1[:]))
+        nc.vector.tensor_copy(wp_s[:].rearrange("p (t q) -> p t q", t=PACK), w_s[:].rearrange("p (q t) -> p t q", t=PACK))
+        nc.vector.tensor_copy(go_w[:], xo_w[:].indirect(l2[:]))
+        nc.vector.tensor_copy(go_s[:], xo_s[:].indirect(l2[:]))
+
+        a_ps = [psum.tile([P, J], F32, name="a_ps%d" % t, tag="bank%d" % t) for t in range(PACK)]
+        b_ps = [psum.tile([P, J], F32, name="b_ps%d" % t, tag="bank%d" % (PACK + t)) for t in range(PACK)]
+        for t in range(PACK):
+            cols = slice(t * P, (t + 1) * P)
+            nc.tensor.matmul_mx(a_ps[t][:], lhsT=wp_w[:, cols].bitcast(E4M3), lhsT_scale=wp_s[:, cols],
+                                rhs=gt_w[:].bitcast(E2M1), rhs_scale=gt_s[:], start=True, stop=True)
+        for t in range(PACK):
+            cols = slice(t * P, (t + 1) * P)
+            nc.tensor.matmul_mx(b_ps[t][:], lhsT=wp_w[:, cols].bitcast(E4M3), lhsT_scale=wp_s[:, cols],
+                                rhs=go_w[:].bitcast(E4M3), rhs_scale=go_s[:], start=True, stop=True)
+
+        a_sb = [sb("a_sb%d" % t, [P, J], F32) for t in range(PACK)]
+        b_sb = [sb("b_sb%d" % t, [P, J], F32) for t in range(PACK)]
+        pg = [sb("pg%d" % t, [P, C], F32) for t in range(PACK)]
+        for t in range(PACK):
+            nc.scalar.activation(a_sb[t][:], a_ps[t][:], COPY)
+            nc.scalar.activation(pw[t][:].indirect(l3[:]), a_sb[t][:], COPY)
+            nc.vector.tensor_copy(b_sb[t][:], b_ps[t][:])
+            nc.vector.tensor_copy(pv[t][:].indirect(l4[:]), b_sb[t][:])
+            adder = nc.vector if t >= 3 else nc.gpsimd
+            adder.tensor_tensor(pg[t][:], pw[t][:], pv[t][:], ADD)
+
+        H = O // 2
+        hid = [sb("hid%d" % h, [P, PACK, H], F32) for h in range(2)]
+        for t in range(PACK):
+            for h in range(2):
+                picked = pg[t][:].indirect(l5[:, h * H // 16 : (h + 1) * H // 16])
+                if t == PACK - 1 and h == 0:
+                    nc.vector.tensor_copy(hid[h][:, t, :], picked)
+                else:
+                    nc.scalar.activation(hid[h][:, t, :], picked, COPY)
+
+        y_ps = [psum.tile([P, O], F32, name="y_ps%d" % n, tag="bank%d" % n) for n in range(N // P)]
+        for h in range(2):
+            hb = sb("hb%d" % h, [P, H, PACK], BF16)
+            dst = hb[:].rearrange("p (c i) t -> p c t i", i=4)
+            src = hid[h][:].rearrange("p t (c i) -> p c t i", i=4)
+            if h == 0:
+                nc.vector.tensor_copy(dst, src)
+            else:
+                nc.scalar.copy(dst, src)
+            hq_w = sb("hq_w%d" % h, [P, H], U32)
+            hq_s = sb("hq_s%d" % h, [P, H], U8)
+            nc.vector.quantize_mx(hq_w[:].bitcast(E5M2), hq_s[:], hb[:].rearrange("p o t -> p (o t)"))
+            for n in range(N // P):
+                nc.tensor.matmul_mx(y_ps[n][:, h * H : (h + 1) * H], lhsT=wb_w[:, 2 * n * P : 2 * (n + 1) * P].bitcast(E2M1),
+                                    lhsT_scale=wb_s[:, n * P : (n + 1) * P],
+                                    rhs=hq_w[:].bitcast(E5M2), rhs_scale=hq_s[:], start=True, stop=True)
+        for n in range(N // P):
+            y = sb("y%d" % n, [P, O], F32)
+            if n == 0:
+                nc.vector.tensor_copy(y[:], y_ps[n][:])
+                nc.sync.dma_start(out[n * P : (n + 1) * P, :], y[:])
+            else:
+                nc.scalar.copy(y[:], y_ps[n][:])
+                nc.scalar.dma_start(out[n * P : (n + 1) * P, :], y[:])

@@ -30,8 +30,8 @@ def tile_list_oneforboth_shared_one_plain_kernel(
         keep = ctx.enter_context(tc.tile_pool(name="keep", bufs=1))
         psum = ctx.enter_context(tc.psum_pool(name="psum", bufs=1))
 
-        def sb(name, shape, dtype):
-            return keep.tile(shape, dtype, name=name, align_bytes=64)
+        def sb(name, shape, dtype, tag=None):
+            return keep.tile(shape, dtype, name=name, tag=tag or name, align_bytes=64)
 
         def load_list(name, src):
             tile = sb(name, [P, J // 16], U16)
@@ -55,18 +55,18 @@ def tile_list_oneforboth_shared_one_plain_kernel(
         xo_w = sb("xo_w", [P, Z], U32)
         wb_w = sb("wb_w", [P, 2 * N], U8)
 
-        nc.sync.dma_start(xt_w[:].bitcast(I32), xt_words[0].bitcast(I32))
         l1 = load_list("l1", offs)
+        nc.sync.dma_start(xt_w[:].bitcast(I32), xt_words[0].bitcast(I32))
+        for r in range(4):
+            load_rows(nc.sync, xt_s, xt_scales, r)
         nc.sync.dma_start(w_w[:].bitcast(I32), w_words[0].rearrange("p n t -> p (n t)").bitcast(I32))
-        for r in range(4):
-            load_rows(nc.scalar if r % 2 else nc.sync, xt_s, xt_scales, r)
-        for r in range(4):
-            load_rows(nc.scalar if r % 2 else nc.sync, w_s, w_scales, r)
         l2 = load_list("l2", offs2)
+        for r in range(4):
+            load_rows(nc.sync, w_s, w_scales, r)
         nc.sync.dma_start(xo_w[:].bitcast(I32), xo_words[0].rearrange("p n t -> p (n t)").bitcast(I32))
-        l3 = load_list("l3", offs3)
         for r in range(4):
             load_rows(nc.sync, xo_s, xo_scales, r)
+        l3 = load_list("l3", offs3)
         l4 = load_list("l4", offs4)
         l5 = load_list("l5", offs5)
         nc.sync.dma_start(wb_w[:].bitcast(I32), wb_words[0].bitcast(I32))
@@ -92,39 +92,74 @@ def tile_list_oneforboth_shared_one_plain_kernel(
         nc.vector.tensor_copy(go_w[:], xo_w[:].indirect(l2[:]))
         nc.vector.tensor_copy(go_s[:], xo_s[:].indirect(l2[:]))
 
-        a_ps = [psum.tile([P, J], F32, name="a_ps%d" % t, tag="bank%d" % t) for t in range(PACK)]
-        b_ps = [psum.tile([P, J], F32, name="b_ps%d" % t, tag="bank%d" % (PACK + t)) for t in range(PACK)]
+        a_ps = [psum.tile([P, J], F32, name="a_ps%d" % t, tag="bank%d" % t) for t in range(2)]
+        b_ps = [psum.tile([P, J], F32, name="b_ps%d" % t, tag="bank%d" % (2 + t)) for t in range(2)]
+        a23_ps = psum.tile([P, 2 * J], F32, name="a23_ps", tag="bank4")
+        b23_ps = psum.tile([P, 2 * J], F32, name="b23_ps", tag="bank5")
+        a_out = [a_ps[0][:], a_ps[1][:], a23_ps[:, :J], a23_ps[:, J:]]
+        b_out = [b_ps[0][:], b_ps[1][:], b23_ps[:, :J], b23_ps[:, J:]]
         for t in range(PACK):
             cols = slice(t * P, (t + 1) * P)
-            nc.tensor.matmul_mx(a_ps[t][:], lhsT=wp_w[:, cols].bitcast(E4M3), lhsT_scale=wp_s[:, cols],
+            nc.tensor.matmul_mx(a_out[t], lhsT=wp_w[:, cols].bitcast(E4M3), lhsT_scale=wp_s[:, cols],
                                 rhs=gt_w[:].bitcast(E2M1), rhs_scale=gt_s[:], start=True, stop=True)
         for t in range(PACK):
             cols = slice(t * P, (t + 1) * P)
-            nc.tensor.matmul_mx(b_ps[t][:], lhsT=wp_w[:, cols].bitcast(E4M3), lhsT_scale=wp_s[:, cols],
+            nc.tensor.matmul_mx(b_out[t], lhsT=wp_w[:, cols].bitcast(E4M3), lhsT_scale=wp_s[:, cols],
                                 rhs=go_w[:].bitcast(E4M3), rhs_scale=go_s[:], start=True, stop=True)
 
-        a_sb = [sb("a_sb%d" % t, [P, J], F32) for t in range(PACK)]
-        b_sb = [sb("b_sb%d" % t, [P, J], F32) for t in range(PACK)]
+        a_sb = sb("a_sb", [P, 2 * J], F32)
+        a23_sb = sb("a23_sb", [P, 2 * J], F32, tag="xo_s")
+        a_in = [a_sb[:, :J], a_sb[:, J:], a23_sb[:, :J], a23_sb[:, J:]]
+        b_sb = sb("b_sb", [P, PACK * J], F32)
         pg = [sb("pg%d" % t, [P, C], F32) for t in range(PACK)]
-        for t in range(PACK):
-            nc.scalar.activation(a_sb[t][:], a_ps[t][:], COPY)
-            nc.scalar.activation(pw[t][:].indirect(l3[:]), a_sb[t][:], COPY)
-            nc.vector.tensor_copy(b_sb[t][:], b_ps[t][:])
-            nc.vector.tensor_copy(pv[t][:].indirect(l4[:]), b_sb[t][:])
-            adder = nc.vector if t >= 3 else nc.gpsimd
-            adder.tensor_tensor(pg[t][:], pw[t][:], pv[t][:], ADD)
-
         H = O // 2
         hid = [sb("hid%d" % h, [P, PACK, H], F32) for h in range(2)]
-        for t in range(PACK):
-            for h in range(2):
-                picked = pg[t][:].indirect(l5[:, h * H // 16 : (h + 1) * H // 16])
-                if t == PACK - 1 and h == 0:
-                    nc.vector.tensor_copy(hid[h][:, t, :], picked)
-                else:
-                    nc.scalar.activation(hid[h][:, t, :], picked, COPY)
 
-        y_ps = [psum.tile([P, O], F32, name="y_ps%d" % n, tag="bank%d" % n) for n in range(N // P)]
+        def place_a(t):
+            nc.scalar.activation(pw[t][:].indirect(l3[:]), a_in[t], COPY)
+
+        def place_b(t):
+            if t == PACK - 1:
+                nc.scalar.activation(pv[t][:].indirect(l4[:]), b_sb[:, t * J : (t + 1) * J], COPY)
+            else:
+                nc.vector.tensor_copy(pv[t][:].indirect(l4[:]), b_sb[:, t * J : (t + 1) * J])
+
+        def add(t):
+            nc.vector.tensor_tensor(pg[t][:], pw[t][:], pv[t][:], ADD)
+
+        def pick(t, h, on_vector):
+            picked = pg[t][:].indirect(l5[:, h * H // 16 : (h + 1) * H // 16])
+            if on_vector:
+                nc.vector.tensor_copy(hid[h][:, t, :], picked)
+            else:
+                nc.scalar.activation(hid[h][:, t, :], picked, COPY)
+
+        nc.scalar.copy(a_sb[:, :J], a_out[0])
+        nc.scalar.copy(a_sb[:, J : 2 * J], a_out[1])
+        place_a(0)
+        nc.vector.tensor_copy(a23_sb[:], a23_ps[:])
+        nc.vector.tensor_copy(b_sb[:, :J], b_out[0])
+        nc.vector.tensor_copy(b_sb[:, J : 2 * J], b_out[1])
+        place_b(0)
+        place_a(1)
+        nc.scalar.copy(b_sb[:, 2 * J :], b23_ps[:])
+        place_b(1)
+        add(0)
+        place_a(2)
+        place_b(2)
+        add(1)
+        place_a(3)
+        add(2)
+        place_b(3)
+        for t in range(2):
+            pick(t, 0, False)
+            pick(t, 1, False)
+        pick(2, 1, False)
+        pick(2, 0, True)
+        add(3)
+        pick(3, 0, True)
+        pick(3, 1, True)
+
         for h in range(2):
             hb = sb("hb%d" % h, [P, H, PACK], BF16)
             dst = hb[:].rearrange("p (c i) t -> p c t i", i=4)
@@ -137,14 +172,14 @@ def tile_list_oneforboth_shared_one_plain_kernel(
             hq_s = sb("hq_s%d" % h, [P, H], U8)
             nc.vector.quantize_mx(hq_w[:].bitcast(E5M2), hq_s[:], hb[:].rearrange("p o t -> p (o t)"))
             for n in range(N // P):
-                nc.tensor.matmul_mx(y_ps[n][:, h * H : (h + 1) * H], lhsT=wb_w[:, 2 * n * P : 2 * (n + 1) * P].bitcast(E2M1),
+                y_ps = psum.tile([P, H], F32, name="y_ps%d%d" % (h, n), tag="bank%d" % (2 * h + n))
+                nc.tensor.matmul_mx(y_ps[:], lhsT=wb_w[:, 2 * n * P : 2 * (n + 1) * P].bitcast(E2M1),
                                     lhsT_scale=wb_s[:, n * P : (n + 1) * P],
                                     rhs=hq_w[:].bitcast(E5M2), rhs_scale=hq_s[:], start=True, stop=True)
-        for n in range(N // P):
-            y = sb("y%d" % n, [P, O], F32)
-            if n == 0:
-                nc.vector.tensor_copy(y[:], y_ps[n][:])
-                nc.sync.dma_start(out[n * P : (n + 1) * P, :], y[:])
-            else:
-                nc.scalar.copy(y[:], y_ps[n][:])
-                nc.scalar.dma_start(out[n * P : (n + 1) * P, :], y[:])
+                y = sb("y%d%d" % (h, n), [P, H], F32)
+                if h == 1 and n == 0:
+                    nc.vector.tensor_copy(y[:], y_ps[:])
+                else:
+                    nc.scalar.copy(y[:], y_ps[:])
+                queue = nc.scalar if h == 1 and n == 1 else nc.sync
+                queue.dma_start(out[n * P : (n + 1) * P, h * H : (h + 1) * H], y[:])

from contextlib import ExitStack

import concourse.mybir as mybir

K, T, Z, J, R, C, O, N = 512, 1024, 1024, 256, 512, 512, 256, 256
FLOPS = 2 * K * R * J * 2 + 2 * R * N * O

F32 = mybir.dt.float32
BF16 = mybir.dt.bfloat16
I32 = mybir.dt.int32
U32 = mybir.dt.uint32
U16 = mybir.dt.uint16
U8 = mybir.dt.uint8
E4M3 = mybir.dt.float8_e4m3fn_x4
E5M2 = mybir.dt.float8_e5m2_x4
E2M1 = mybir.dt.float4_e2m1fn_x4
COPY = mybir.ActivationFunctionType.Copy
ADD = mybir.AluOpType.add

P = 128
PACK = 4


def tile_list_oneforboth_shared_one_plain_kernel(
    tc, xt_words, xt_scales, xo_words, xo_scales, w_words, w_scales, wb_words, wb_scales,
    offs, offs2, offs3, offs4, offs5, out,
):
    nc = tc.nc
    with ExitStack() as ctx:
        keep = ctx.enter_context(tc.tile_pool(name="keep", bufs=1))
        psum = ctx.enter_context(tc.psum_pool(name="psum", bufs=1))

        def sb(name, shape, dtype, tag=None):
            return keep.tile(shape, dtype, name=name, tag=tag or name, align_bytes=64)

        def load_list(name, src):
            tile = sb(name, [P, J // 16], U16)
            nc.sync.dma_start(tile[:], src)
            return tile

        def new_plane(name, width):
            plane = sb(name, [P, width], U8)
            nc.vector.memset(plane[:].bitcast(I32), 0)
            return plane

        def load_rows(queue, plane, src, r):
            queue.dma_start(plane[r:P:32, :].bitcast(I32), src[0, r:16:4, :].bitcast(I32))

        xt_s = new_plane("xt_s", T)
        w_s = new_plane("w_s", R)
        xo_s = new_plane("xo_s", Z)
        wb_s = new_plane("wb_s", N)
        xt_w = sb("xt_w", [P, T], U16)
        w_w = sb("w_w", [P, R], U32)
        xo_w = sb("xo_w", [P, Z], U32)
        wb_w = sb("wb_w", [P, 2 * N], U8)

        l1 = load_list("l1", offs)
        nc.sync.dma_start(xt_w[:].bitcast(I32), xt_words[0].bitcast(I32))
        for r in range(4):
            load_rows(nc.sync, xt_s, xt_scales, r)
        nc.sync.dma_start(w_w[:].bitcast(I32), w_words[0].rearrange("p n t -> p (n t)").bitcast(I32))
        l2 = load_list("l2", offs2)
        for r in range(4):
            load_rows(nc.sync, w_s, w_scales, r)
        nc.sync.dma_start(xo_w[:].bitcast(I32), xo_words[0].rearrange("p n t -> p (n t)").bitcast(I32))
        for r in range(4):
            load_rows(nc.sync, xo_s, xo_scales, r)
        l3 = load_list("l3", offs3)
        l4 = load_list("l4", offs4)
        l5 = load_list("l5", offs5)
        nc.sync.dma_start(wb_w[:].bitcast(I32), wb_words[0].bitcast(I32))
        for r in range(4):
            load_rows(nc.sync, wb_s, wb_scales, r)

        pw = [sb("pw%d" % t, [P, C], F32) for t in range(PACK)]
        pv = [sb("pv%d" % t, [P, C], F32) for t in range(PACK)]
        for t in range(PACK):
            nc.vector.memset(pw[t][:], 0.0)
            nc.vector.memset(pv[t][:], 0.0)

        wp_w = sb("wp_w", [P, R], U32)
        wp_s = sb("wp_s", [P, R], U8)
        gt_w = sb("gt_w", [P, J], U16)
        gt_s = sb("gt_s", [P, J], U8)
        go_w = sb("go_w", [P, J], U32)
        go_s = sb("go_s", [P, J], U8)
        nc.scalar.copy(wp_w[:].rearrange("p (t q) -> p t q", t=PACK), w_w[:].rearrange("p (q t) -> p t q", t=PACK))
        nc.vector.tensor_copy(gt_w[:], xt_w[:].indirect(l1[:]))
        nc.vector.tensor_copy(gt_s[:], xt_s[:].indirect(l1[:]))
        nc.vector.tensor_copy(wp_s[:].rearrange("p (t q) -> p t q", t=PACK), w_s[:].rearrange("p (q t) -> p t q", t=PACK))
        nc.vector.tensor_copy(go_w[:], xo_w[:].indirect(l2[:]))
        nc.vector.tensor_copy(go_s[:], xo_s[:].indirect(l2[:]))

        a_ps = [psum.tile([P, J], F32, name="a_ps%d" % t, tag="bank%d" % t) for t in range(2)]
        b_ps = [psum.tile([P, J], F32, name="b_ps%d" % t, tag="bank%d" % (2 + t)) for t in range(2)]
        a23_ps = psum.tile([P, 2 * J], F32, name="a23_ps", tag="bank4")
        b23_ps = psum.tile([P, 2 * J], F32, name="b23_ps", tag="bank5")
        a_out = [a_ps[0][:], a_ps[1][:], a23_ps[:, :J], a23_ps[:, J:]]
        b_out = [b_ps[0][:], b_ps[1][:], b23_ps[:, :J], b23_ps[:, J:]]
        for t in range(PACK):
            cols = slice(t * P, (t + 1) * P)
            nc.tensor.matmul_mx(a_out[t], lhsT=wp_w[:, cols].bitcast(E4M3), lhsT_scale=wp_s[:, cols],
                                rhs=gt_w[:].bitcast(E2M1), rhs_scale=gt_s[:], start=True, stop=True)
        for t in range(PACK):
            cols = slice(t * P, (t + 1) * P)
            nc.tensor.matmul_mx(b_out[t], lhsT=wp_w[:, cols].bitcast(E4M3), lhsT_scale=wp_s[:, cols],
                                rhs=go_w[:].bitcast(E4M3), rhs_scale=go_s[:], start=True, stop=True)

        a_sb = sb("a_sb", [P, 2 * J], F32)
        a23_sb = sb("a23_sb", [P, 2 * J], F32, tag="xo_s")
        a_in = [a_sb[:, :J], a_sb[:, J:], a23_sb[:, :J], a23_sb[:, J:]]
        b_sb = sb("b_sb", [P, PACK * J], F32)
        pg = [sb("pg%d" % t, [P, C], F32) for t in range(PACK)]
        H = O // 2
        hid = [sb("hid%d" % h, [P, PACK, H], F32) for h in range(2)]

        def place_a(t):
            nc.scalar.activation(pw[t][:].indirect(l3[:]), a_in[t], COPY)

        def place_b(t):
            if t == PACK - 1:
                nc.scalar.activation(pv[t][:].indirect(l4[:]), b_sb[:, t * J : (t + 1) * J], COPY)
            else:
                nc.vector.tensor_copy(pv[t][:].indirect(l4[:]), b_sb[:, t * J : (t + 1) * J])

        def add(t):
            nc.vector.tensor_tensor(pg[t][:], pw[t][:], pv[t][:], ADD)

        def pick(t, h, on_vector):
            picked = pg[t][:].indirect(l5[:, h * H // 16 : (h + 1) * H // 16])
            if on_vector:
                nc.vector.tensor_copy(hid[h][:, t, :], picked)
            else:
                nc.scalar.activation(hid[h][:, t, :], picked, COPY)

        nc.scalar.copy(a_sb[:, :J], a_out[0])
        nc.scalar.copy(a_sb[:, J : 2 * J], a_out[1])
        place_a(0)
        nc.vector.tensor_copy(a23_sb[:], a23_ps[:])
        nc.vector.tensor_copy(b_sb[:, :J], b_out[0])
        nc.vector.tensor_copy(b_sb[:, J : 2 * J], b_out[1])
        place_b(0)
        place_a(1)
        nc.scalar.copy(b_sb[:, 2 * J :], b23_ps[:])
        place_b(1)
        add(0)
        place_a(2)
        place_b(2)
        add(1)
        place_a(3)
        add(2)
        place_b(3)
        for t in range(2):
            pick(t, 0, False)
            pick(t, 1, False)
        pick(2, 1, False)
        pick(2, 0, True)
        add(3)
        pick(3, 0, True)
        pick(3, 1, True)

        for h in range(2):
            hb = sb("hb%d" % h, [P, H, PACK], BF16)
            dst = hb[:].rearrange("p (c i) t -> p c t i", i=4)
            src = hid[h][:].rearrange("p t (c i) -> p c t i", i=4)
            if h == 0:
                nc.vector.tensor_copy(dst, src)
            else:
                nc.scalar.copy(dst, src)
            hq_w = sb("hq_w%d" % h, [P, H], U32)
            hq_s = sb("hq_s%d" % h, [P, H], U8)
            nc.vector.quantize_mx(hq_w[:].bitcast(E5M2), hq_s[:], hb[:].rearrange("p o t -> p (o t)"))
            for n in range(N // P):
                y_ps = psum.tile([P, H], F32, name="y_ps%d%d" % (h, n), tag="bank%d" % (2 * h + n))
                nc.tensor.matmul_mx(y_ps[:], lhsT=wb_w[:, 2 * n * P : 2 * (n + 1) * P].bitcast(E2M1),
                                    lhsT_scale=wb_s[:, n * P : (n + 1) * P],
                                    rhs=hq_w[:].bitcast(E5M2), rhs_scale=hq_s[:], start=True, stop=True)
                y = sb("y%d%d" % (h, n), [P, H], F32)
                if h == 1 and n == 0:
                    nc.vector.tensor_copy(y[:], y_ps[:])
                else:
                    nc.scalar.copy(y[:], y_ps[:])
                queue = nc.scalar if h == 1 and n == 1 else nc.sync
                queue.dma_start(out[n * P : (n + 1) * P, h * H : (h + 1) * H], y[:])
